import numpy as np
import ml_dtypes


def mxq(x, axis, fmt="e4m3"):
    dtype, down = {"e4m3": (ml_dtypes.float8_e4m3fn, 7), "e5m2": (ml_dtypes.float8_e5m2, 14)}[fmt]
    v = np.moveaxis(np.asarray(x, np.float32).astype(ml_dtypes.bfloat16).astype(np.float64), axis, -1)
    blocks = v.reshape(v.shape[:-1] + (-1, 32))
    amax = np.abs(blocks).max(-1, keepdims=True)
    byte = np.maximum(np.where(amax > 0, np.frexp(amax)[1] - 1 + 127, 0) - down, 1)
    scale = np.exp2(byte - 127.0)
    codes = (blocks / scale).astype(np.float32).astype(dtype).astype(np.float64)
    return np.moveaxis((codes * scale).reshape(v.shape), -1, axis)


WIDE = False


def mx_kscale(k):
    if not WIDE:
        return np.ones(k)
    levels = np.array([10, -10, 5, -5, 0])
    if k % 512:
        return np.exp2(np.random.permutation(np.resize(levels, k // 32))).repeat(32)
    a = np.empty((k // 512, 16))
    for p in range(k // 512):
        a[p, :8] = np.random.permutation(np.resize(levels, 8))
        for g in range(8):
            far = levels[np.abs(levels - a[p, g]) >= 10]
            a[p, g + 8] = far[np.random.randint(len(far))]
    return np.exp2(a.ravel()).repeat(32)


def f64(x):
    return np.asarray(x).astype(np.float64)


def striped(idx):
    return np.tile(idx.reshape(-1, 16).T, (8, 1)).astype(np.uint16)


def unstriped(offs):
    return offs[:16].T.reshape(-1).astype(np.int64)


E2M1 = np.array([0.0, 0.5, 1.0, 1.5, 2.0, 3.0, 4.0, 6.0, -0.0, -0.5, -1.0, -1.5, -2.0, -3.0, -4.0, -6.0])


def pack_weight(w, fmt):
    k, n = w.shape
    w = f64(np.asarray(w, np.float32).astype(ml_dtypes.bfloat16)).reshape(k // 32, 32, n)
    amax = np.abs(w).max(1)
    if fmt == "e4m3":
        byte = np.frexp(amax)[1] - 1 + 127 - 7
    else:
        mant, ex = np.frexp(amax / 6.0)
        byte = np.where(mant > 0.5, ex, ex - 1) + 127
    byte = np.clip(np.where(amax > 0, byte, 1), 1, 254)
    scaled = (w * np.exp2(127.0 - byte)[:, None, :]).reshape(k, n).astype(np.float32)
    by_word = np.ascontiguousarray(scaled.reshape(k // 512, 128, 4, n).transpose(0, 1, 3, 2))
    if fmt == "e4m3":
        words = by_word.astype(ml_dtypes.float8_e4m3fn).view(np.uint8)
    else:
        c = by_word.astype(ml_dtypes.float4_e2m1fn).view(np.uint8) & 0xF
        words = (c[..., 0::2] | (c[..., 1::2] << 4)).reshape(k // 512, 128, 2 * n)
    return np.ascontiguousarray(words), np.ascontiguousarray(byte.astype(np.uint8).reshape(k // 512, 16, n))


def unpack_weight(words, scales, fmt):
    g, _, n = scales.shape
    words = np.ascontiguousarray(words).reshape(g, 128, n, -1)
    if fmt == "e4m3":
        vals = words.view(ml_dtypes.float8_e4m3fn).astype(np.float64)
    else:
        nib = np.empty((g, 128, n, 4), np.uint8)
        nib[..., 0::2] = words & 0xF
        nib[..., 1::2] = words >> 4
        vals = E2M1[nib]
    vals = vals * np.repeat(np.exp2(scales.astype(np.float64) - 127.0), 8, axis=1)[..., None]
    return vals.transpose(0, 1, 3, 2).reshape(g * 512, n)


def d_relu(v):
    return (v > 0).astype(np.float64)


K, T, E, C, H, N = 128, 1024, 12, 256, 512, 512
TOP = 3


def by_expert(wq, xq):
    return np.concatenate([wq[e].T @ xq[:, e * C:(e + 1) * C] for e in range(E)], axis=1)


def setup_inputs():
    n = np.random.standard_normal
    s = mx_kscale(N)[:, None]
    u = mx_kscale(H)
    deal = np.repeat(np.arange(E), C).reshape(TOP, T)[:, np.random.permutation(T)]
    deal = np.take_along_axis(deal, np.argsort(np.random.rand(TOP, T), axis=0), axis=0)
    for _ in range(8):
        s_, t_ = np.random.permutation(T).reshape(2, -1); r = np.random.randint(TOP, size=T // 2); x, y = deal[r, s_].copy(), deal[r, t_].copy()
        ok = ~((deal[:, s_] == y).any(0) | (deal[:, t_] == x).any(0)); deal[r[ok], s_[ok]] = y[ok]; deal[r[ok], t_[ok]] = x[ok]
    order = np.lexsort((np.random.rand(TOP * T), deal.reshape(-1)))
    slot_token = order % T; pos = np.empty(TOP * T, np.int64); pos[order] = np.arange(TOP * T); pos = pos.reshape(TOP, T)
    g = np.random.uniform(0.5, 1.5, (TOP, T)); g = g / g.sum(0)
    w_slot = np.empty(E * C)
    for r in range(TOP): w_slot[pos[r]] = g[r]
    w2 = [pack_weight(m, "e2m1") for m in n((E, N, H)) / np.sqrt(N) / s[None] * u[None, None, :]]
    w1 = [pack_weight(m, "e2m1") for m in n((E, H, K)) / np.sqrt(H) / u[None, :, None]]
    return {
        "dyT": (n((N, T)) * s).astype(np.float32),
        "a": n((H, E * C)).astype(np.float32),
        "w2_words": np.stack([m[0] for m in w2]),
        "w2_scales": np.stack([m[1] for m in w2]),
        "w1_words": np.stack([m[0] for m in w1]),
        "w1_scales": np.stack([m[1] for m in w1]),
        "gate": np.tile(w_slot, (N, 1)).astype(np.float32),
        "offs": striped(slot_token),
        "pos1": striped(pos[0]),
        "pos2": striped(pos[1]),
        "pos3": striped(pos[2]),
    }


def reference(dyT, a, w2_words, w2_scales, w1_words, w1_scales, gate, offs, pos1, pos2, pos3):
    idx = unstriped(offs)
    w2 = np.stack([unpack_weight(w2_words[e], w2_scales[e], "e2m1") for e in range(E)])
    w1 = np.stack([unpack_weight(w1_words[e], w1_scales[e], "e2m1") for e in range(E)])
    gq = mxq(f64(gate) * f64(dyT)[:, idx], 0, "e4m3")
    dh = by_expert(w2, gq)
    da = dh * d_relu(f64(a))
    dx = by_expert(w1, mxq(da, 0, "e4m3"))
    return dx[:, unstriped(pos1)] + dx[:, unstriped(pos2)] + dx[:, unstriped(pos3)]

@@ -1,0 +1,277 @@
+from contextlib import ExitStack
+
+import concourse.mybir as mybir
+from concourse.masks import make_identity
+
+K, T, E, C, H, N = 128, 1024, 12, 256, 512, 512
+S = E * C
+P = 128
+FLOPS = 2 * S * N * H + 2 * S * H * K
+F32 = mybir.dt.float32
+BF16 = mybir.dt.bfloat16
+U32 = mybir.dt.uint32
+I32 = mybir.dt.int32
+U16 = mybir.dt.uint16
+U8 = mybir.dt.uint8
+FP8X4 = mybir.dt.float8_e4m3fn_x4
+FP4X4 = mybir.dt.float4_e2m1fn_x4
+ALU = mybir.AluOpType
+ACT = mybir.ActivationFunctionType
+
+CHUNKS = [2,2,2,2,2,2]
+MODES = "111111111111"
+PIECES = [640,384]
+LAG_Q1, LAG_MM1, LAG_T, LAG_MASK, LAG_Q2, LAG_OUT = 2, 2, 5, 6, 7, 8
+
+
+def tile_moe_bdx_mlp_relu_kernel(
+    tc, dyT, a, w2_words, w2_scales, w1_words, w1_scales, gate, offs, pos1, pos2, pos3, out
+):
+    nc = tc.nc
+    with ExitStack() as ctx:
+        keep = ctx.enter_context(tc.tile_pool(name="keep", bufs=1))
+        ring = ctx.enter_context(tc.tile_pool(name="ring", bufs=3))
+        psum = ctx.enter_context(tc.psum_pool(name="psum", bufs=2))
+
+        offs_sb = keep.tile([P, S // 16], U16, name="offs_sb")
+        pos_sb = [keep.tile([P, T // 16], U16, name="pos%d" % r) for r in range(3)]
+        dy = [keep.tile([P, T], F32, name="dy%d" % t) for t in range(4)]
+        starts = [sum(CHUNKS[:c]) for c in range(len(CHUNKS))]
+        gate_sb = [keep.tile([P, n * C], F32, name="gate%d" % c) for c, n in enumerate(CHUNKS)]
+        a_sb = [keep.tile([P, 4, n * C], F32, name="a%d" % c) for c, n in enumerate(CHUNKS)]
+        w2_sb = [keep.tile([P, n, 2 * H], U8, name="w2_%d" % c, align_bytes=64) for c, n in enumerate(CHUNKS)]
+        w1_sb = keep.tile([P, E, 2 * K], U8, name="w1_sb", align_bytes=64)
+        s2 = keep.tile([P, E, H], U8, name="s2", align_bytes=64)
+        s1 = keep.tile([P, E, K], U8, name="s1", align_bytes=64)
+        dx = keep.tile([P, S], F32, name="dx")
+        ident_f = keep.tile([P, P], F32, name="ident_f")
+        make_identity(nc, ident_f[:])
+        if "1" in MODES:
+            ident_b = keep.tile([P, P], BF16, name="ident_b")
+            make_identity(nc, ident_b[:])
+        nc.vector.memset(s2[:].rearrange("p e n -> p (e n)").bitcast(I32), 0)
+        nc.vector.memset(s1[:].rearrange("p e n -> p (e n)").bitcast(I32), 0)
+
+        dy_h = dyT.rearrange("(p t) s -> p t s", t=4)
+        a_h = a.rearrange("(p t) s -> p t s", t=4)
+        w2_h = w2_words.bitcast(I32)
+        w1_h = w1_words.bitcast(I32)
+        s2_h = w2_scales.bitcast(I32)
+        s1_h = w1_scales.bitcast(I32)
+
+        def load_gate(c, q=nc.sync):
+            q.dma_start(gate_sb[c][:], gate[0:P, starts[c] * C : (starts[c] + CHUNKS[c]) * C])
+
+        def load_a(c):
+            nc.sync.dma_start(a_sb[c][:], a_h[:, :, starts[c] * C : (starts[c] + CHUNKS[c]) * C])
+
+        def load_w2(c):
+            nc.sync.dma_start(
+                w2_sb[c][:].bitcast(I32),
+                w2_h[starts[c] : starts[c] + CHUNKS[c], 0].rearrange("e p b -> p e b"),
+            )
+
+        def load_scales(plane, src):
+            for q in range(4):
+                nc.sync.dma_start(
+                    plane[32 * q : 32 * q + 4].bitcast(I32),
+                    src[:, 0, 4 * q : 4 * q + 4, :].rearrange("e r b -> r e b"),
+                )
+
+        nc.sync.dma_start(dy[0][:], dy_h[:, 0, :])
+        nc.sync.dma_start(offs_sb[:], offs)
+        load_gate(0, nc.scalar)
+        for t in range(1, 4):
+            nc.sync.dma_start(dy[t][:], dy_h[:, t, :])
+        load_gate(1)
+        load_w2(0)
+        load_scales(s2, s2_h)
+        load_a(0)
+        load_gate(2)
+        load_scales(s1, s1_h)
+        nc.sync.dma_start(w1_sb[:].bitcast(I32), w1_h[:, 0].rearrange("e p b -> p e b"))
+        for c in range(1, len(CHUNKS)):
+            load_w2(c)
+            load_a(c)
+            if c + 2 < len(CHUNKS):
+                load_gate(c + 2)
+        for r, pos in enumerate((pos1, pos2, pos3)):
+            nc.sync.dma_start(pos_sb[r][:], pos)
+
+        chunk_of = [c for c, n in enumerate(CHUNKS) for j in range(n)]
+        g4 = {}
+        gb = {}
+        gq = {}
+        dhT = {}
+        pw = {}
+        da = {}
+        dq = {}
+        sg = {}
+        p2 = {}
+
+        def gather(c, t):
+            n = CHUNKS[c] * C
+            if t == 0:
+                g4[c] = ring.tile([P, 4, n], F32, name="g4", bufs=3)
+            cols = slice(starts[c] * C // 16, (starts[c] * C + n) // 16)
+            nc.vector.tensor_tensor(g4[c][:, t, :], dy[t][:].indirect(offs_sb[:, cols]), gate_sb[c][:], ALU.mult)
+
+        def local(e):
+            c = chunk_of[e]
+            j = e - starts[c]
+            return c, slice(j * C, (j + 1) * C)
+
+        def round_g(e):
+            c, sl = local(e)
+            gb[e] = ring.tile([P, C, 4], BF16, name="gb", align_bytes=64, bufs=4)
+            nc.scalar.copy(
+                gb[e][:].rearrange("p (c i) t -> p c t i", i=4),
+                g4[c][:, :, sl].rearrange("p t (c i) -> p c t i", i=4),
+            )
+
+        def quant(store, src, e, name):
+            codes = ring.tile([P, C], U32, name=name + "c", align_bytes=64)
+            scales = ring.tile([P, C], U8, name=name + "s", align_bytes=64)
+            nc.vector.quantize_mx(codes[:].bitcast(FP8X4), scales[:], src[e][:].rearrange("p s t -> p (s t)"))
+            store[e] = (codes, scales)
+
+        def mm1(e):
+            c = chunk_of[e]
+            j = e - starts[c]
+            codes, scales = gq[e]
+            dhT[e] = []
+            for h in range(2):
+                p1 = psum.tile([P, H], F32, name="p1", bufs=4)
+                sl = slice(h * P, (h + 1) * P)
+                nc.tensor.matmul_mx(
+                    p1[:], lhsT=codes[:, sl].bitcast(FP8X4), lhsT_scale=scales[:, sl],
+                    rhs=w2_sb[c][:, j, :].bitcast(FP4X4), rhs_scale=s2[:, e, :], start=True, stop=True,
+                )
+                d = ring.tile([P, H], BF16, name="dhT", bufs=10)
+                if MODES[e] == "1":
+                    nc.scalar.copy(d[:].rearrange("s (t p) -> s t p", t=4), p1[:].rearrange("s (p t) -> s t p", t=4))
+                else:
+                    nc.scalar.copy(
+                        d[:].rearrange("s (u p e) -> s u p e", u=2, e=2),
+                        p1[:].rearrange("s (p u e) -> s u p e", u=2, e=2),
+                    )
+                dhT[e].append(d)
+
+        def turn(e):
+            pw[e] = psum.tile([P, 2 * C], F32, name="pw")
+            for h in range(2):
+                d = dhT[e][h]
+                if MODES[e] == "1":
+                    view = pw[e][:].bitcast(BF16).rearrange("p (t s) -> p t s", t=4)
+                    for t in range(4):
+                        nc.tensor.transpose(view[:, t, h * P : (h + 1) * P], d[:, t * P : (t + 1) * P], ident_b[:])
+                else:
+                    words = d[:].bitcast(F32)
+                    for u in range(2):
+                        nc.tensor.transpose(
+                            pw[e][:, u * C + h * P : u * C + (h + 1) * P], words[:, u * P : (u + 1) * P], ident_f[:]
+                        )
+
+        def sign(e):
+            c, sl = local(e)
+            if MODES[e] == "3":
+                sg[e] = ring.tile([P, C, 4], BF16, name="sg")
+                nc.scalar.activation(
+                    sg[e][:].rearrange("p (c i) t -> p c t i", i=4),
+                    a_sb[c][:, :, sl].rearrange("p t (c i) -> p c t i", i=4),
+                    ACT.Sign,
+                )
+
+        def step01(e):
+            if MODES[e] == "3":
+                m = ring.tile([P, C * 4], BF16, name="m01")
+                nc.vector.tensor_scalar(m[:], sg[e][:].rearrange("p s t -> p (s t)"), 0.0, None, ALU.max)
+                sg[e] = m
+
+        def mask(e):
+            c, sl = local(e)
+            da[e] = ring.tile([P, C, 4], BF16, name="da", align_bytes=64)
+            if MODES[e] == "1":
+                nc.vector.scalar_tensor_tensor(
+                    da[e][:], a_sb[c][:, :, sl].rearrange("p t s -> p s t"), 0.0,
+                    pw[e][:].bitcast(BF16).rearrange("p (t s) -> p s t", t=4), ALU.is_gt, ALU.mult,
+                )
+            elif MODES[e] == "2":
+                half = ring.tile([P, 2, C, 2], BF16, name="half")
+                for u in range(2):
+                    nc.vector.scalar_tensor_tensor(
+                        half[:, u], a_sb[c][:, 2 * u : 2 * u + 2, sl].rearrange("p e s -> p s e"), 0.0,
+                        pw[e][:, u * C : (u + 1) * C].bitcast(BF16).rearrange("p (s e) -> p s e", e=2),
+                        ALU.is_gt, ALU.mult,
+                    )
+                nc.scalar.copy(
+                    da[e][:].rearrange("p s t -> p (s t)").bitcast(F32).rearrange("p (s u) -> p s u", u=2),
+                    half[:].rearrange("p u s e -> p (u s e)").bitcast(F32).rearrange("p (u s) -> p s u", u=2),
+                )
+            else:
+                nc.vector.tensor_tensor(
+                    da[e][:].rearrange("p s (u e) -> p s u e", u=2),
+                    pw[e][:].bitcast(BF16).rearrange("p (u s e) -> p s u e", u=2, e=2),
+                    sg[e][:].rearrange("p (s u e) -> p s u e", u=2, e=2),
+                    ALU.mult,
+                )
+
+        def mm2(e):
+            codes, scales = dq[e]
+            p2[e] = psum.tile([P, C], F32, name="p2")
+            nc.tensor.matmul_mx(
+                p2[e][:], lhsT=w1_sb[:, e, :].bitcast(FP4X4), lhsT_scale=s1[:, e, :],
+                rhs=codes[:].bitcast(FP8X4), rhs_scale=scales[:], start=True, stop=True,
+            )
+            nc.scalar.copy(dx[:, e * C : (e + 1) * C], p2[e][:])
+
+        todo = [(c, t) for c in range(len(CHUNKS)) for t in range(4)]
+        done = 0
+
+        def ok(e):
+            return 0 <= e < E
+
+        for k in range(E + LAG_OUT):
+            want = 0
+            if k < E:
+                c = chunk_of[k]
+                want = 4 * c + (4 * (k - starts[c] + 1)) // CHUNKS[c]
+            mine = todo[done:max(want, done)]
+            done = max(want, done)
+            half_n = (len(mine) + 1) // 2
+            if ok(k - LAG_MASK):
+                mask(k - LAG_MASK)
+            for c, t in mine[:half_n]:
+                gather(c, t)
+            if ok(k - LAG_Q1):
+                quant(gq, gb, k - LAG_Q1, "gq")
+            if ok(k - LAG_MM1):
+                mm1(k - LAG_MM1)
+            if ok(k - LAG_Q2):
+                quant(dq, da, k - LAG_Q2, "dq")
+            if ok(k - LAG_MASK + 1):
+                step01(k - LAG_MASK + 1)
+            for c, t in mine[half_n:]:
+                gather(c, t)
+            if k < E and k + 1 == starts[chunk_of[k]] + CHUNKS[chunk_of[k]]:
+                for e in range(starts[chunk_of[k]], k + 1):
+                    round_g(e)
+            if ok(k - LAG_T):
+                turn(k - LAG_T)
+            if ok(k - LAG_OUT + 1):
+                mm2(k - LAG_OUT + 1)
+            if ok(k - LAG_MASK + 2):
+                sign(k - LAG_MASK + 2)
+
+        t0 = 0
+        for i, n in enumerate(PIECES):
+            cols = slice(t0 // 16, (t0 + n) // 16)
+            got = [keep.tile([P, n], F32, name="got%d_%d" % (i, r)) for r in range(3)]
+            for r in range(3):
+                nc.vector.tensor_copy(got[r][:], dx[:].indirect(pos_sb[r][:, cols]))
+            two = keep.tile([P, n], F32, name="two%d" % i)
+            res = keep.tile([P, n], F32, name="res%d" % i)
+            nc.vector.tensor_tensor(two[:], got[0][:], got[1][:], ALU.add)
+            (nc.vector).tensor_tensor(res[:], two[:], got[2][:], ALU.add)
+            nc.sync.dma_start(out[:, t0 : t0 + n], res[:])
+            t0 += n

@@ -19,9 +19,10 @@ ALU = mybir.AluOpType
 ACT = mybir.ActivationFunctionType
 
 CHUNKS = [2,2,2,2,2,2]
-MODES = "111111111111"
+MODES = "322223"
+ALIAS = [None,None,None,None,1,None]
+SIGN_AT = [0,1,2,4,2,3]
 PIECES = [640,384]
-LAG_Q1, LAG_MM1, LAG_T, LAG_MASK, LAG_Q2, LAG_OUT = 2, 2, 5, 6, 7, 8
 
 
 def tile_moe_bdx_mlp_relu_kernel(
@@ -45,12 +46,10 @@ def tile_moe_bdx_mlp_relu_kernel(
         s1 = keep.tile([P, E, K], U8, name="s1", align_bytes=64)
         dx = keep.tile([P, S], F32, name="dx")
         ident_f = keep.tile([P, P], F32, name="ident_f")
-        make_identity(nc, ident_f[:])
-        if "1" in MODES:
-            ident_b = keep.tile([P, P], BF16, name="ident_b")
-            make_identity(nc, ident_b[:])
         nc.vector.memset(s2[:].rearrange("p e n -> p (e n)").bitcast(I32), 0)
         nc.vector.memset(s1[:].rearrange("p e n -> p (e n)").bitcast(I32), 0)
+
+        make_identity(nc, ident_f[:])
 
         dy_h = dyT.rearrange("(p t) s -> p t s", t=4)
         a_h = a.rearrange("(p t) s -> p t s", t=4)
@@ -75,7 +74,7 @@ def tile_moe_bdx_mlp_relu_kernel(
             for q in range(4):
                 nc.sync.dma_start(
                     plane[32 * q : 32 * q + 4].bitcast(I32),
-                    src[:, 0, 4 * q : 4 * q + 4, :].rearrange("e r b -> r e b"),
+                    src[:, 4 * q : 4 * q + 4, :].rearrange("e r b -> r e b"),
                 )
 
         nc.sync.dma_start(dy[0][:], dy_h[:, 0, :])
@@ -83,22 +82,32 @@ def tile_moe_bdx_mlp_relu_kernel(
         load_gate(0, nc.scalar)
         for t in range(1, 4):
             nc.sync.dma_start(dy[t][:], dy_h[:, t, :])
-        load_gate(1)
-        load_w2(0)
-        load_scales(s2, s2_h)
-        load_a(0)
+        load_w2(3)
         load_gate(2)
-        load_scales(s1, s1_h)
+        load_gate(1)
+        load_a(0)
+        load_scales(s2[:, 0:4, :], s2_h[0:4, 0])
+        load_scales(s1[:], s1_h[:, 0])
+        load_a(1)
+        load_gate(3)
+        load_w2(0)
+        load_w2(5)
+        load_w2(1)
+        load_a(2)
+        load_scales(s2[:, 4:8, :], s2_h[4:8, 0])
         nc.sync.dma_start(w1_sb[:].bitcast(I32), w1_h[:, 0].rearrange("e p b -> p e b"))
-        for c in range(1, len(CHUNKS)):
-            load_w2(c)
-            load_a(c)
-            if c + 2 < len(CHUNKS):
-                load_gate(c + 2)
+        load_scales(s2[:, 8:12, :], s2_h[8:12, 0])
+        load_a(5)
+        load_gate(5)
+        load_gate(4)
+        load_w2(2)
+        load_a(4)
+        load_a(3)
+        load_w2(4)
         for r, pos in enumerate((pos1, pos2, pos3)):
             nc.sync.dma_start(pos_sb[r][:], pos)
 
-        chunk_of = [c for c, n in enumerate(CHUNKS) for j in range(n)]
+        NC = len(CHUNKS)
         g4 = {}
         gb = {}
         gq = {}
@@ -107,161 +116,142 @@ def tile_moe_bdx_mlp_relu_kernel(
         da = {}
         dq = {}
         sg = {}
-        p2 = {}
 
         def gather(c, t):
             n = CHUNKS[c] * C
             if t == 0:
-                g4[c] = ring.tile([P, 4, n], F32, name="g4", bufs=3)
+                if ALIAS[c] is None:
+                    g4[c] = ring.tile([P, 4, n], F32, name="g4", bufs=3)
+                else:
+                    g4[c] = a_sb[ALIAS[c]][:, :, 0:n]
             cols = slice(starts[c] * C // 16, (starts[c] * C + n) // 16)
             nc.vector.tensor_tensor(g4[c][:, t, :], dy[t][:].indirect(offs_sb[:, cols]), gate_sb[c][:], ALU.mult)
 
-        def local(e):
-            c = chunk_of[e]
-            j = e - starts[c]
-            return c, slice(j * C, (j + 1) * C)
-
-        def round_g(e):
-            c, sl = local(e)
-            gb[e] = ring.tile([P, C, 4], BF16, name="gb", align_bytes=64, bufs=4)
+        def round_g(c):
+            gb[c] = ring.tile([P, CHUNKS[c] * C, 4], BF16, name="gb", align_bytes=64, bufs=4)
             nc.scalar.copy(
-                gb[e][:].rearrange("p (c i) t -> p c t i", i=4),
-                g4[c][:, :, sl].rearrange("p t (c i) -> p c t i", i=4),
+                gb[c][:].rearrange("p (c i) t -> p c t i", i=4),
+                g4[c][:, :, :].rearrange("p t (c i) -> p c t i", i=4),
             )
 
-        def quant(store, src, e, name):
-            codes = ring.tile([P, C], U32, name=name + "c", align_bytes=64)
-            scales = ring.tile([P, C], U8, name=name + "s", align_bytes=64)
-            nc.vector.quantize_mx(codes[:].bitcast(FP8X4), scales[:], src[e][:].rearrange("p s t -> p (s t)"))
-            store[e] = (codes, scales)
+        def quant(store, src, c, name, bufs):
+            n = CHUNKS[c] * C
+            codes = ring.tile([P, n], U32, name=name + "c", align_bytes=64, bufs=bufs)
+            scales = ring.tile([P, n], U8, name=name + "s", align_bytes=64, bufs=bufs)
+            nc.vector.quantize_mx(codes[:].bitcast(FP8X4), scales[:], src[c][:].rearrange("p s t -> p (s t)"))
+            store[c] = (codes, scales)
 
-        def mm1(e):
-            c = chunk_of[e]
-            j = e - starts[c]
-            codes, scales = gq[e]
-            dhT[e] = []
-            for h in range(2):
+        def mm1(c):
+            codes, scales = gq[c]
+            dhT[c] = []
+            for h in range(2 * CHUNKS[c]):
                 p1 = psum.tile([P, H], F32, name="p1", bufs=4)
                 sl = slice(h * P, (h + 1) * P)
                 nc.tensor.matmul_mx(
                     p1[:], lhsT=codes[:, sl].bitcast(FP8X4), lhsT_scale=scales[:, sl],
-                    rhs=w2_sb[c][:, j, :].bitcast(FP4X4), rhs_scale=s2[:, e, :], start=True, stop=True,
+                    rhs=w2_sb[c][:, h // 2, :].bitcast(FP4X4), rhs_scale=s2[:, starts[c] + h // 2, :],
+                    start=True, stop=True,
                 )
-                d = ring.tile([P, H], BF16, name="dhT", bufs=10)
-                if MODES[e] == "1":
-                    nc.scalar.copy(d[:].rearrange("s (t p) -> s t p", t=4), p1[:].rearrange("s (p t) -> s t p", t=4))
-                else:
-                    nc.scalar.copy(
-                        d[:].rearrange("s (u p e) -> s u p e", u=2, e=2),
-                        p1[:].rearrange("s (p u e) -> s u p e", u=2, e=2),
-                    )
-                dhT[e].append(d)
+                d = ring.tile([P, H], BF16, name="dhT", bufs=12)
+                nc.scalar.copy(
+                    d[:].rearrange("s (u p e) -> s u p e", u=2, e=2),
+                    p1[:].rearrange("s (p u e) -> s u p e", u=2, e=2),
+                )
+                dhT[c].append(d)
 
-        def turn(e):
-            pw[e] = psum.tile([P, 2 * C], F32, name="pw")
+        def turn(c, j):
+            pw[c, j] = psum.tile([P, 2 * C], F32, name="pw")
             for h in range(2):
-                d = dhT[e][h]
-                if MODES[e] == "1":
-                    view = pw[e][:].bitcast(BF16).rearrange("p (t s) -> p t s", t=4)
-                    for t in range(4):
-                        nc.tensor.transpose(view[:, t, h * P : (h + 1) * P], d[:, t * P : (t + 1) * P], ident_b[:])
-                else:
-                    words = d[:].bitcast(F32)
-                    for u in range(2):
-                        nc.tensor.transpose(
-                            pw[e][:, u * C + h * P : u * C + (h + 1) * P], words[:, u * P : (u + 1) * P], ident_f[:]
-                        )
+                words = dhT[c][2 * j + h][:].bitcast(F32)
+                for u in range(2):
+                    nc.tensor.transpose(
+                        pw[c, j][:, u * C + h * P : u * C + (h + 1) * P], words[:, u * P : (u + 1) * P], ident_f[:]
+                    )
 
-        def sign(e):
-            c, sl = local(e)
-            if MODES[e] == "3":
-                sg[e] = ring.tile([P, C, 4], BF16, name="sg")
+        def sign(c):
+            if MODES[c] == "3":
+                sg[c] = ring.tile([P, CHUNKS[c] * C, 4], BF16, name="sg", bufs=3)
                 nc.scalar.activation(
-                    sg[e][:].rearrange("p (c i) t -> p c t i", i=4),
-                    a_sb[c][:, :, sl].rearrange("p t (c i) -> p c t i", i=4),
+                    sg[c][:].rearrange("p (c i) t -> p c t i", i=4),
+                    a_sb[c][:].rearrange("p t (c i) -> p c t i", i=4),
                     ACT.Sign,
                 )
 
-        def step01(e):
-            if MODES[e] == "3":
-                m = ring.tile([P, C * 4], BF16, name="m01")
-                nc.vector.tensor_scalar(m[:], sg[e][:].rearrange("p s t -> p (s t)"), 0.0, None, ALU.max)
-                sg[e] = m
+        def step01(c):
+            if MODES[c] == "3":
+                m = ring.tile([P, CHUNKS[c] * C * 4], BF16, name="m01")
+                nc.vector.tensor_scalar(m[:], sg[c][:].rearrange("p s t -> p (s t)"), 0.0, None, ALU.max)
+                sg[c] = m
 
-        def mask(e):
-            c, sl = local(e)
-            da[e] = ring.tile([P, C, 4], BF16, name="da", align_bytes=64)
-            if MODES[e] == "1":
-                nc.vector.scalar_tensor_tensor(
-                    da[e][:], a_sb[c][:, :, sl].rearrange("p t s -> p s t"), 0.0,
-                    pw[e][:].bitcast(BF16).rearrange("p (t s) -> p s t", t=4), ALU.is_gt, ALU.mult,
-                )
-            elif MODES[e] == "2":
+        def mask(c, j):
+            sl = slice(j * C, (j + 1) * C)
+            if j == 0:
+                da[c] = ring.tile([P, CHUNKS[c] * C, 4], BF16, name="da", align_bytes=64)
+            if MODES[c] == "2":
                 half = ring.tile([P, 2, C, 2], BF16, name="half")
                 for u in range(2):
                     nc.vector.scalar_tensor_tensor(
                         half[:, u], a_sb[c][:, 2 * u : 2 * u + 2, sl].rearrange("p e s -> p s e"), 0.0,
-                        pw[e][:, u * C : (u + 1) * C].bitcast(BF16).rearrange("p (s e) -> p s e", e=2),
+                        pw[c, j][:, u * C : (u + 1) * C].bitcast(BF16).rearrange("p (s e) -> p s e", e=2),
                         ALU.is_gt, ALU.mult,
                     )
                 nc.scalar.copy(
-                    da[e][:].rearrange("p s t -> p (s t)").bitcast(F32).rearrange("p (s u) -> p s u", u=2),
+                    da[c][:, sl, :].rearrange("p s t -> p (s t)").bitcast(F32).rearrange("p (s u) -> p s u", u=2),
                     half[:].rearrange("p u s e -> p (u s e)").bitcast(F32).rearrange("p (u s) -> p s u", u=2),
                 )
             else:
                 nc.vector.tensor_tensor(
-                    da[e][:].rearrange("p s (u e) -> p s u e", u=2),
-                    pw[e][:].bitcast(BF16).rearrange("p (u s e) -> p s u e", u=2, e=2),
-                    sg[e][:].rearrange("p (s u e) -> p s u e", u=2, e=2),
+                    da[c][:, sl, :].rearrange("p s (u e) -> p s u e", u=2),
+                    pw[c, j][:].bitcast(BF16).rearrange("p (u s e) -> p s u e", u=2, e=2),
+                    sg[c][:, j * 4 * C : (j + 1) * 4 * C].rearrange("p (s u e) -> p s u e", u=2, e=2),
                     ALU.mult,
                 )
 
-        def mm2(e):
-            codes, scales = dq[e]
-            p2[e] = psum.tile([P, C], F32, name="p2")
-            nc.tensor.matmul_mx(
-                p2[e][:], lhsT=w1_sb[:, e, :].bitcast(FP4X4), lhsT_scale=s1[:, e, :],
-                rhs=codes[:].bitcast(FP8X4), rhs_scale=scales[:], start=True, stop=True,
-            )
-            nc.scalar.copy(dx[:, e * C : (e + 1) * C], p2[e][:])
+        def mm2(c):
+            codes, scales = dq[c]
+            n = CHUNKS[c] * C
+            p2 = psum.tile([P, n], F32, name="p2")
+            for j in range(CHUNKS[c]):
+                e = starts[c] + j
+                sl = slice(j * C, (j + 1) * C)
+                nc.tensor.matmul_mx(
+                    p2[:, sl], lhsT=w1_sb[:, e, :].bitcast(FP4X4), lhsT_scale=s1[:, e, :],
+                    rhs=codes[:, sl].bitcast(FP8X4), rhs_scale=scales[:, sl], start=True, stop=True,
+                )
+            nc.scalar.copy(dx[:, starts[c] * C : starts[c] * C + n], p2[:])
 
-        todo = [(c, t) for c in range(len(CHUNKS)) for t in range(4)]
-        done = 0
+        LAG = 3
 
-        def ok(e):
-            return 0 <= e < E
+        def ok(c):
+            return 0 <= c < NC
 
-        for k in range(E + LAG_OUT):
-            want = 0
-            if k < E:
-                c = chunk_of[k]
-                want = 4 * c + (4 * (k - starts[c] + 1)) // CHUNKS[c]
-            mine = todo[done:max(want, done)]
-            done = max(want, done)
-            half_n = (len(mine) + 1) // 2
-            if ok(k - LAG_MASK):
-                mask(k - LAG_MASK)
-            for c, t in mine[:half_n]:
-                gather(c, t)
-            if ok(k - LAG_Q1):
-                quant(gq, gb, k - LAG_Q1, "gq")
-            if ok(k - LAG_MM1):
-                mm1(k - LAG_MM1)
-            if ok(k - LAG_Q2):
-                quant(dq, da, k - LAG_Q2, "dq")
-            if ok(k - LAG_MASK + 1):
-                step01(k - LAG_MASK + 1)
-            for c, t in mine[half_n:]:
-                gather(c, t)
-            if k < E and k + 1 == starts[chunk_of[k]] + CHUNKS[chunk_of[k]]:
-                for e in range(starts[chunk_of[k]], k + 1):
-                    round_g(e)
-            if ok(k - LAG_T):
-                turn(k - LAG_T)
-            if ok(k - LAG_OUT + 1):
-                mm2(k - LAG_OUT + 1)
-            if ok(k - LAG_MASK + 2):
-                sign(k - LAG_MASK + 2)
+        for k in range(NC + LAG + 1):
+            m = k - LAG
+            if ok(m):
+                for j in range(CHUNKS[m]):
+                    mask(m, j)
+            if ok(k):
+                gather(k, 0)
+                gather(k, 1)
+            if ok(k - 1):
+                quant(gq, gb, k - 1, "gq", 2)
+                mm1(k - 1)
+            if ok(k):
+                gather(k, 2)
+            if ok(m):
+                quant(dq, da, m, "dq", 3)
+                mm2(m)
+            if ok(m + 1):
+                step01(m + 1)
+            if ok(k):
+                gather(k, 3)
+                round_g(k)
+            if ok(m + 1):
+                for j in range(CHUNKS[m + 1]):
+                    turn(m + 1, j)
+            for c in range(NC):
+                if SIGN_AT[c] == k:
+                    sign(c)
 
         t0 = 0
         for i, n in enumerate(PIECES):

@@ -261,7 +261,7 @@ def tile_moe_bdx_mlp_relu_kernel(
                 nc.vector.tensor_copy(got[r][:], dx[:].indirect(pos_sb[r][:, cols]))
             two = keep.tile([P, n], F32, name="two%d" % i)
             res = keep.tile([P, n], F32, name="res%d" % i)
-            nc.vector.tensor_tensor(two[:], got[0][:], got[1][:], ALU.add)
-            (nc.vector).tensor_tensor(res[:], two[:], got[2][:], ALU.add)
+            nc.gpsimd.tensor_tensor(two[:], got[0][:], got[1][:], ALU.add)
+            (nc.gpsimd if i + 1 < len(PIECES) else nc.vector).tensor_tensor(res[:], two[:], got[2][:], ALU.add)
             nc.sync.dma_start(out[:, t0 : t0 + n], res[:])
             t0 += n

@@ -253,15 +253,35 @@ def tile_moe_bdx_mlp_relu_kernel(
                 if SIGN_AT[c] == k:
                     sign(c)
 
-        t0 = 0
-        for i, n in enumerate(PIECES):
-            cols = slice(t0 // 16, (t0 + n) // 16)
-            got = [keep.tile([P, n], F32, name="got%d_%d" % (i, r)) for r in range(3)]
-            for r in range(3):
-                nc.vector.tensor_copy(got[r][:], dx[:].indirect(pos_sb[r][:, cols]))
-            two = keep.tile([P, n], F32, name="two%d" % i)
-            res = keep.tile([P, n], F32, name="res%d" % i)
-            nc.gpsimd.tensor_tensor(two[:], got[0][:], got[1][:], ALU.add)
-            (nc.gpsimd if i + 1 < len(PIECES) else nc.vector).tensor_tensor(res[:], two[:], got[2][:], ALU.add)
-            nc.sync.dma_start(out[:, t0 : t0 + n], res[:])
-            t0 += n
+        NB = 5
+        TA = NB * P
+        TB = T - TA
+        got_a = [keep.tile([P, TA], F32, name="got_a%d" % r) for r in range(3)]
+        got_b = [keep.tile([P, TB], F32, name="got_b%d" % r) for r in range(3)]
+        sums = [psum.tile([P, H], F32, name="p1", bufs=4) for b in range(4)] + [psum.tile([P, H], F32, name="p2")]
+        for r in range(3):
+            nc.vector.tensor_copy(got_a[r][:], dx[:].indirect(pos_sb[r][:, 0 : TA // 16]))
+            for b in range(NB):
+                nc.tensor.matmul(
+                    sums[b][:, 0:P], lhsT=got_a[r][:, b * P : (b + 1) * P], rhs=ident_f[:],
+                    start=(r == 0), stop=(r == 2), is_transpose=True,
+                )
+        turned = keep.tile([P, TA], F32, name="turned")
+        first = keep.tile([P, TA], F32, name="first")
+        for b0, b1 in ((0, 3), (3, NB)):
+            back = psum.tile([P, 2 * C], F32, name="pw")
+            for b in range(b0, b1):
+                nc.scalar.copy(turned[:, b * P : (b + 1) * P], sums[b][:, 0:P])
+                nc.tensor.transpose(back[:, (b - b0) * P : (b - b0 + 1) * P], turned[:, b * P : (b + 1) * P], ident_f[:])
+            nc.scalar.copy(first[:, b0 * P : b1 * P], back[:, 0 : (b1 - b0) * P])
+            nc.scalar.dma_start(out[:, b0 * P : b1 * P], first[:, b0 * P : b1 * P])
+        for r in range(3):
+            nc.vector.tensor_copy(got_b[r][:], dx[:].indirect(pos_sb[r][:, TA // 16 : T // 16]))
+        halves = [slice(i * TB // 2, (i + 1) * TB // 2) for i in range(2)]
+        two = [keep.tile([P, TB // 2], F32, name="two%d" % i) for i in range(2)]
+        for i in range(2):
+            nc.vector.tensor_tensor(two[i][:], got_b[0][:, halves[i]], got_b[1][:, halves[i]], ALU.add)
+        for i in range(2):
+            res = keep.tile([P, TB // 2], F32, name="res%d" % i)
+            nc.vector.tensor_tensor(res[:], two[i][:], got_b[2][:, halves[i]], ALU.add)
+            nc.sync.dma_start(out[:, TA + halves[i].start : TA + halves[i].stop], res[:])

@@ -19,9 +19,9 @@ ALU = mybir.AluOpType
 ACT = mybir.ActivationFunctionType
 
 CHUNKS = [2,2,2,2,2,2]
-MODES = "322223"
-ALIAS = [None,None,None,None,1,None]
-SIGN_AT = [0,1,2,4,2,3]
+MODES = "323223"
+ALIAS = [None,None,None,None,None,None]
+SIGN_AT = [1,1,2,4,3,4]
 PIECES = [640,384]
 
 
@@ -82,28 +82,28 @@ def tile_moe_bdx_mlp_relu_kernel(
         load_gate(0, nc.scalar)
         for t in range(1, 4):
             nc.sync.dma_start(dy[t][:], dy_h[:, t, :])
-        load_w2(3)
         load_gate(2)
         load_gate(1)
-        load_a(0)
-        load_scales(s2[:, 0:4, :], s2_h[0:4, 0])
-        load_scales(s1[:], s1_h[:, 0])
-        load_a(1)
-        load_gate(3)
-        load_w2(0)
-        load_w2(5)
-        load_w2(1)
-        load_a(2)
-        load_scales(s2[:, 4:8, :], s2_h[4:8, 0])
-        nc.sync.dma_start(w1_sb[:].bitcast(I32), w1_h[:, 0].rearrange("e p b -> p e b"))
-        load_scales(s2[:, 8:12, :], s2_h[8:12, 0])
-        load_a(5)
-        load_gate(5)
-        load_gate(4)
-        load_w2(2)
-        load_a(4)
-        load_a(3)
         load_w2(4)
+        load_a(0)
+        load_w2(1)
+        load_scales(s2[:, 4:8, :], s2_h[4:8, 0])
+        load_a(3)
+        load_scales(s2[:, 8:12, :], s2_h[8:12, 0])
+        load_w2(3)
+        load_w2(0)
+        load_scales(s1[:], s1_h[:, 0])
+        load_scales(s2[:, 0:4, :], s2_h[0:4, 0])
+        load_gate(3)
+        load_a(5)
+        load_a(1)
+        load_w2(2)
+        load_w2(5)
+        nc.sync.dma_start(w1_sb[:].bitcast(I32), w1_h[:, 0].rearrange("e p b -> p e b"))
+        load_a(4)
+        load_gate(4)
+        load_a(2)
+        load_gate(5)
         for r, pos in enumerate((pos1, pos2, pos3)):
             nc.sync.dma_start(pos_sb[r][:], pos)
 
@@ -128,7 +128,7 @@ def tile_moe_bdx_mlp_relu_kernel(
             nc.vector.tensor_tensor(g4[c][:, t, :], dy[t][:].indirect(offs_sb[:, cols]), gate_sb[c][:], ALU.mult)
 
         def round_g(c):
-            gb[c] = ring.tile([P, CHUNKS[c] * C, 4], BF16, name="gb", align_bytes=64, bufs=4)
+            gb[c] = ring.tile([P, CHUNKS[c] * C, 4], BF16, name="gb", align_bytes=64, bufs=3)
             nc.scalar.copy(
                 gb[c][:].rearrange("p (c i) t -> p c t i", i=4),
                 g4[c][:, :, :].rearrange("p t (c i) -> p c t i", i=4),
@@ -170,7 +170,7 @@ def tile_moe_bdx_mlp_relu_kernel(
 
         def sign(c):
             if MODES[c] == "3":
-                sg[c] = ring.tile([P, CHUNKS[c] * C, 4], BF16, name="sg", bufs=3)
+                sg[c] = ring.tile([P, CHUNKS[c] * C, 4], BF16, name="sg", bufs=2)
                 nc.scalar.activation(
                     sg[c][:].rearrange("p (c i) t -> p c t i", i=4),
                     a_sb[c][:].rearrange("p t (c i) -> p c t i", i=4),

from contextlib import ExitStack

import concourse.mybir as mybir
from concourse.masks import make_identity

K, T, E, C, H, N = 128, 1024, 12, 256, 512, 512
S = E * C
P = 128
FLOPS = 2 * S * N * H + 2 * S * H * K
F32 = mybir.dt.float32
BF16 = mybir.dt.bfloat16
U32 = mybir.dt.uint32
I32 = mybir.dt.int32
U16 = mybir.dt.uint16
U8 = mybir.dt.uint8
FP8X4 = mybir.dt.float8_e4m3fn_x4
FP4X4 = mybir.dt.float4_e2m1fn_x4
ALU = mybir.AluOpType
ACT = mybir.ActivationFunctionType

CHUNKS = [2,2,2,2,2,2]
MODES = "323223"
ALIAS = [None,None,None,None,None,None]
SIGN_AT = [1,1,2,4,3,4]
PIECES = [640,384]


def tile_moe_bdx_mlp_relu_kernel(
    tc, dyT, a, w2_words, w2_scales, w1_words, w1_scales, gate, offs, pos1, pos2, pos3, out
):
    nc = tc.nc
    with ExitStack() as ctx:
        keep = ctx.enter_context(tc.tile_pool(name="keep", bufs=1))
        ring = ctx.enter_context(tc.tile_pool(name="ring", bufs=3))
        psum = ctx.enter_context(tc.psum_pool(name="psum", bufs=2))

        offs_sb = keep.tile([P, S // 16], U16, name="offs_sb")
        pos_sb = [keep.tile([P, T // 16], U16, name="pos%d" % r) for r in range(3)]
        dy = [keep.tile([P, T], F32, name="dy%d" % t) for t in range(4)]
        starts = [sum(CHUNKS[:c]) for c in range(len(CHUNKS))]
        gate_sb = [keep.tile([P, n * C], F32, name="gate%d" % c) for c, n in enumerate(CHUNKS)]
        a_sb = [keep.tile([P, 4, n * C], F32, name="a%d" % c) for c, n in enumerate(CHUNKS)]
        w2_sb = [keep.tile([P, n, 2 * H], U8, name="w2_%d" % c, align_bytes=64) for c, n in enumerate(CHUNKS)]
        w1_sb = keep.tile([P, E, 2 * K], U8, name="w1_sb", align_bytes=64)
        s2 = keep.tile([P, E, H], U8, name="s2", align_bytes=64)
        s1 = keep.tile([P, E, K], U8, name="s1", align_bytes=64)
        dx = keep.tile([P, S], F32, name="dx")
        ident_f = keep.tile([P, P], F32, name="ident_f")
        nc.vector.memset(s2[:].rearrange("p e n -> p (e n)").bitcast(I32), 0)
        nc.vector.memset(s1[:].rearrange("p e n -> p (e n)").bitcast(I32), 0)

        make_identity(nc, ident_f[:])

        dy_h = dyT.rearrange("(p t) s -> p t s", t=4)
        a_h = a.rearrange("(p t) s -> p t s", t=4)
        w2_h = w2_words.bitcast(I32)
        w1_h = w1_words.bitcast(I32)
        s2_h = w2_scales.bitcast(I32)
        s1_h = w1_scales.bitcast(I32)

        def load_gate(c, q=nc.sync):
            q.dma_start(gate_sb[c][:], gate[0:P, starts[c] * C : (starts[c] + CHUNKS[c]) * C])

        def load_a(c):
            nc.sync.dma_start(a_sb[c][:], a_h[:, :, starts[c] * C : (starts[c] + CHUNKS[c]) * C])

        def load_w2(c):
            nc.sync.dma_start(
                w2_sb[c][:].bitcast(I32),
                w2_h[starts[c] : starts[c] + CHUNKS[c], 0].rearrange("e p b -> p e b"),
            )

        def load_scales(plane, src):
            for q in range(4):
                nc.sync.dma_start(
                    plane[32 * q : 32 * q + 4].bitcast(I32),
                    src[:, 4 * q : 4 * q + 4, :].rearrange("e r b -> r e b"),
                )

        nc.sync.dma_start(dy[0][:], dy_h[:, 0, :])
        nc.sync.dma_start(offs_sb[:], offs)
        load_gate(0, nc.scalar)
        for t in range(1, 4):
            nc.sync.dma_start(dy[t][:], dy_h[:, t, :])
        load_gate(2)
        load_gate(1)
        load_w2(4)
        load_a(0)
        load_w2(1)
        load_scales(s2[:, 4:8, :], s2_h[4:8, 0])
        load_a(3)
        load_scales(s2[:, 8:12, :], s2_h[8:12, 0])
        load_w2(3)
        load_w2(0)
        load_scales(s1[:], s1_h[:, 0])
        load_scales(s2[:, 0:4, :], s2_h[0:4, 0])
        load_gate(3)
        load_a(5)
        load_a(1)
        load_w2(2)
        load_w2(5)
        nc.sync.dma_start(w1_sb[:].bitcast(I32), w1_h[:, 0].rearrange("e p b -> p e b"))
        load_a(4)
        load_gate(4)
        load_a(2)
        load_gate(5)
        for r, pos in enumerate((pos1, pos2, pos3)):
            nc.sync.dma_start(pos_sb[r][:], pos)

        NC = len(CHUNKS)
        g4 = {}
        gb = {}
        gq = {}
        dhT = {}
        pw = {}
        da = {}
        dq = {}
        sg = {}

        def gather(c, t):
            n = CHUNKS[c] * C
            if t == 0:
                if ALIAS[c] is None:
                    g4[c] = ring.tile([P, 4, n], F32, name="g4", bufs=3)
                else:
                    g4[c] = a_sb[ALIAS[c]][:, :, 0:n]
            cols = slice(starts[c] * C // 16, (starts[c] * C + n) // 16)
            nc.vector.tensor_tensor(g4[c][:, t, :], dy[t][:].indirect(offs_sb[:, cols]), gate_sb[c][:], ALU.mult)

        def round_g(c):
            gb[c] = ring.tile([P, CHUNKS[c] * C, 4], BF16, name="gb", align_bytes=64, bufs=3)
            nc.scalar.copy(
                gb[c][:].rearrange("p (c i) t -> p c t i", i=4),
                g4[c][:, :, :].rearrange("p t (c i) -> p c t i", i=4),
            )

        def quant(store, src, c, name, bufs):
            n = CHUNKS[c] * C
            codes = ring.tile([P, n], U32, name=name + "c", align_bytes=64, bufs=bufs)
            scales = ring.tile([P, n], U8, name=name + "s", align_bytes=64, bufs=bufs)
            nc.vector.quantize_mx(codes[:].bitcast(FP8X4), scales[:], src[c][:].rearrange("p s t -> p (s t)"))
            store[c] = (codes, scales)

        def mm1(c):
            codes, scales = gq[c]
            dhT[c] = []
            for h in range(2 * CHUNKS[c]):
                p1 = psum.tile([P, H], F32, name="p1", bufs=4)
                sl = slice(h * P, (h + 1) * P)
                nc.tensor.matmul_mx(
                    p1[:], lhsT=codes[:, sl].bitcast(FP8X4), lhsT_scale=scales[:, sl],
                    rhs=w2_sb[c][:, h // 2, :].bitcast(FP4X4), rhs_scale=s2[:, starts[c] + h // 2, :],
                    start=True, stop=True,
                )
                d = ring.tile([P, H], BF16, name="dhT", bufs=12)
                nc.scalar.copy(
                    d[:].rearrange("s (u p e) -> s u p e", u=2, e=2),
                    p1[:].rearrange("s (p u e) -> s u p e", u=2, e=2),
                )
                dhT[c].append(d)

        def turn(c, j):
            pw[c, j] = psum.tile([P, 2 * C], F32, name="pw")
            for h in range(2):
                words = dhT[c][2 * j + h][:].bitcast(F32)
                for u in range(2):
                    nc.tensor.transpose(
                        pw[c, j][:, u * C + h * P : u * C + (h + 1) * P], words[:, u * P : (u + 1) * P], ident_f[:]
                    )

        def sign(c):
            if MODES[c] == "3":
                sg[c] = ring.tile([P, CHUNKS[c] * C, 4], BF16, name="sg", bufs=2)
                nc.scalar.activation(
                    sg[c][:].rearrange("p (c i) t -> p c t i", i=4),
                    a_sb[c][:].rearrange("p t (c i) -> p c t i", i=4),
                    ACT.Sign,
                )

        def step01(c):
            if MODES[c] == "3":
                m = ring.tile([P, CHUNKS[c] * C * 4], BF16, name="m01")
                nc.vector.tensor_scalar(m[:], sg[c][:].rearrange("p s t -> p (s t)"), 0.0, None, ALU.max)
                sg[c] = m

        def mask(c, j):
            sl = slice(j * C, (j + 1) * C)
            if j == 0:
                da[c] = ring.tile([P, CHUNKS[c] * C, 4], BF16, name="da", align_bytes=64)
            if MODES[c] == "2":
                half = ring.tile([P, 2, C, 2], BF16, name="half")
                for u in range(2):
                    nc.vector.scalar_tensor_tensor(
                        half[:, u], a_sb[c][:, 2 * u : 2 * u + 2, sl].rearrange("p e s -> p s e"), 0.0,
                        pw[c, j][:, u * C : (u + 1) * C].bitcast(BF16).rearrange("p (s e) -> p s e", e=2),
                        ALU.is_gt, ALU.mult,
                    )
                nc.scalar.copy(
                    da[c][:, sl, :].rearrange("p s t -> p (s t)").bitcast(F32).rearrange("p (s u) -> p s u", u=2),
                    half[:].rearrange("p u s e -> p (u s e)").bitcast(F32).rearrange("p (u s) -> p s u", u=2),
                )
            else:
                nc.vector.tensor_tensor(
                    da[c][:, sl, :].rearrange("p s (u e) -> p s u e", u=2),
                    pw[c, j][:].bitcast(BF16).rearrange("p (u s e) -> p s u e", u=2, e=2),
                    sg[c][:, j * 4 * C : (j + 1) * 4 * C].rearrange("p (s u e) -> p s u e", u=2, e=2),
                    ALU.mult,
                )

        def mm2(c):
            codes, scales = dq[c]
            n = CHUNKS[c] * C
            p2 = psum.tile([P, n], F32, name="p2")
            for j in range(CHUNKS[c]):
                e = starts[c] + j
                sl = slice(j * C, (j + 1) * C)
                nc.tensor.matmul_mx(
                    p2[:, sl], lhsT=w1_sb[:, e, :].bitcast(FP4X4), lhsT_scale=s1[:, e, :],
                    rhs=codes[:, sl].bitcast(FP8X4), rhs_scale=scales[:, sl], start=True, stop=True,
                )
            nc.scalar.copy(dx[:, starts[c] * C : starts[c] * C + n], p2[:])

        LAG = 3

        def ok(c):
            return 0 <= c < NC

        for k in range(NC + LAG + 1):
            m = k - LAG
            if ok(m):
                for j in range(CHUNKS[m]):
                    mask(m, j)
            if ok(k):
                gather(k, 0)
                gather(k, 1)
            if ok(k - 1):
                quant(gq, gb, k - 1, "gq", 2)
                mm1(k - 1)
            if ok(k):
                gather(k, 2)
            if ok(m):
                quant(dq, da, m, "dq", 3)
                mm2(m)
            if ok(m + 1):
                step01(m + 1)
            if ok(k):
                gather(k, 3)
                round_g(k)
            if ok(m + 1):
                for j in range(CHUNKS[m + 1]):
                    turn(m + 1, j)
            for c in range(NC):
                if SIGN_AT[c] == k:
                    sign(c)

        NB = 5
        TA = NB * P
        TB = T - TA
        got_a = [keep.tile([P, TA], F32, name="got_a%d" % r) for r in range(3)]
        got_b = [keep.tile([P, TB], F32, name="got_b%d" % r) for r in range(3)]
        sums = [psum.tile([P, H], F32, name="p1", bufs=4) for b in range(4)] + [psum.tile([P, H], F32, name="p2")]
        for r in range(3):
            nc.vector.tensor_copy(got_a[r][:], dx[:].indirect(pos_sb[r][:, 0 : TA // 16]))
            for b in range(NB):
                nc.tensor.matmul(
                    sums[b][:, 0:P], lhsT=got_a[r][:, b * P : (b + 1) * P], rhs=ident_f[:],
                    start=(r == 0), stop=(r == 2), is_transpose=True,
                )
        turned = keep.tile([P, TA], F32, name="turned")
        first = keep.tile([P, TA], F32, name="first")
        for b0, b1 in ((0, 3), (3, NB)):
            back = psum.tile([P, 2 * C], F32, name="pw")
            for b in range(b0, b1):
                nc.scalar.copy(turned[:, b * P : (b + 1) * P], sums[b][:, 0:P])
                nc.tensor.transpose(back[:, (b - b0) * P : (b - b0 + 1) * P], turned[:, b * P : (b + 1) * P], ident_f[:])
            nc.scalar.copy(first[:, b0 * P : b1 * P], back[:, 0 : (b1 - b0) * P])
            nc.scalar.dma_start(out[:, b0 * P : b1 * P], first[:, b0 * P : b1 * P])
        for r in range(3):
            nc.vector.tensor_copy(got_b[r][:], dx[:].indirect(pos_sb[r][:, TA // 16 : T // 16]))
        halves = [slice(i * TB // 2, (i + 1) * TB // 2) for i in range(2)]
        two = [keep.tile([P, TB // 2], F32, name="two%d" % i) for i in range(2)]
        for i in range(2):
            nc.vector.tensor_tensor(two[i][:], got_b[0][:, halves[i]], got_b[1][:, halves[i]], ALU.add)
        for i in range(2):
            res = keep.tile([P, TB // 2], F32, name="res%d" % i)
            nc.vector.tensor_tensor(res[:], two[i][:], got_b[2][:, halves[i]], ALU.add)
            nc.sync.dma_start(out[:, TA + halves[i].start : TA + halves[i].stop], res[:])
